import numpy as np
import ml_dtypes


def mxq(x, axis, fmt="e4m3"):
    dtype, down = {"e4m3": (ml_dtypes.float8_e4m3fn, 7), "e5m2": (ml_dtypes.float8_e5m2, 14)}[fmt]
    v = np.moveaxis(np.asarray(x, np.float32).astype(ml_dtypes.bfloat16).astype(np.float64), axis, -1)
    blocks = v.reshape(v.shape[:-1] + (-1, 32))
    amax = np.abs(blocks).max(-1, keepdims=True)
    byte = np.maximum(np.where(amax > 0, np.frexp(amax)[1] - 1 + 127, 0) - down, 1)
    scale = np.exp2(byte - 127.0)
    codes = (blocks / scale).astype(np.float32).astype(dtype).astype(np.float64)
    return np.moveaxis((codes * scale).reshape(v.shape), -1, axis)


WIDE = False


def mx_kscale(k):
    if not WIDE:
        return np.ones(k)
    levels = np.array([10, -10, 5, -5, 0])
    if k % 512:
        return np.exp2(np.random.permutation(np.resize(levels, k // 32))).repeat(32)
    a = np.empty((k // 512, 16))
    for p in range(k // 512):
        a[p, :8] = np.random.permutation(np.resize(levels, 8))
        for g in range(8):
            far = levels[np.abs(levels - a[p, g]) >= 10]
            a[p, g + 8] = far[np.random.randint(len(far))]
    return np.exp2(a.ravel()).repeat(32)


def f64(x):
    return np.asarray(x).astype(np.float64)


def striped(idx):
    return np.tile(idx.reshape(-1, 16).T, (8, 1)).astype(np.uint16)


def unstriped(offs):
    return offs[:16].T.reshape(-1).astype(np.int64)


E2M1 = np.array([0.0, 0.5, 1.0, 1.5, 2.0, 3.0, 4.0, 6.0, -0.0, -0.5, -1.0, -1.5, -2.0, -3.0, -4.0, -6.0])


def pack_weight(w, fmt):
    k, n = w.shape
    w = f64(np.asarray(w, np.float32).astype(ml_dtypes.bfloat16)).reshape(k // 32, 32, n)
    amax = np.abs(w).max(1)
    if fmt == "e4m3":
        byte = np.frexp(amax)[1] - 1 + 127 - 7
    else:
        mant, ex = np.frexp(amax / 6.0)
        byte = np.where(mant > 0.5, ex, ex - 1) + 127
    byte = np.clip(np.where(amax > 0, byte, 1), 1, 254)
    scaled = (w * np.exp2(127.0 - byte)[:, None, :]).reshape(k, n).astype(np.float32)
    by_word = np.ascontiguousarray(scaled.reshape(k // 512, 128, 4, n).transpose(0, 1, 3, 2))
    if fmt == "e4m3":
        words = by_word.astype(ml_dtypes.float8_e4m3fn).view(np.uint8)
    else:
        c = by_word.astype(ml_dtypes.float4_e2m1fn).view(np.uint8) & 0xF
        words = (c[..., 0::2] | (c[..., 1::2] << 4)).reshape(k // 512, 128, 2 * n)
    return np.ascontiguousarray(words), np.ascontiguousarray(byte.astype(np.uint8).reshape(k // 512, 16, n))


def unpack_weight(words, scales, fmt):
    g, _, n = scales.shape
    words = np.ascontiguousarray(words).reshape(g, 128, n, -1)
    if fmt == "e4m3":
        vals = words.view(ml_dtypes.float8_e4m3fn).astype(np.float64)
    else:
        nib = np.empty((g, 128, n, 4), np.uint8)
        nib[..., 0::2] = words & 0xF
        nib[..., 1::2] = words >> 4
        vals = E2M1[nib]
    vals = vals * np.repeat(np.exp2(scales.astype(np.float64) - 127.0), 8, axis=1)[..., None]
    return vals.transpose(0, 1, 3, 2).reshape(g * 512, n)


def relu(v):
    return np.maximum(v, 0.0)


K, T, E, C, N = 512, 640, 15, 128, 384
TOP = 3


def by_expert(wq, xq):
    return np.concatenate([wq[e].T @ xq[:, e * C:(e + 1) * C] for e in range(E)], axis=1)


def setup_inputs():
    n = np.random.standard_normal
    s = mx_kscale(K)[:, None]
    deal = np.repeat(np.arange(E), C).reshape(TOP, T)[:, np.random.permutation(T)]
    deal = np.take_along_axis(deal, np.argsort(np.random.rand(TOP, T), axis=0), axis=0)
    for _ in range(8):
        s_, t_ = np.random.permutation(T).reshape(2, -1); r = np.random.randint(TOP, size=T // 2); x, y = deal[r, s_].copy(), deal[r, t_].copy()
        ok = ~((deal[:, s_] == y).any(0) | (deal[:, t_] == x).any(0)); deal[r[ok], s_[ok]] = y[ok]; deal[r[ok], t_[ok]] = x[ok]
    order = np.lexsort((np.random.rand(TOP * T), deal.reshape(-1)))
    slot_token = order % T; pos = np.empty(TOP * T, np.int64); pos[order] = np.arange(TOP * T); pos = pos.reshape(TOP, T)
    g = np.random.uniform(0.5, 1.5, (TOP, T)); g = g / g.sum(0)
    x = pack_weight(n((K, T)) * s, "e4m3")
    return {
        "x_words": x[0],
        "x_scales": x[1],
        "w": (n((E, K, N)) / np.sqrt(K) / s[None]).astype(np.float32),
        "b": (0.3 * n((N, E))).astype(np.float32),
        "gate": np.stack([np.tile(r, (N, 1)) for r in g]).astype(np.float32),
        "offs": striped(slot_token),
        "pos1": striped(pos[0]),
        "pos2": striped(pos[1]),
        "pos3": striped(pos[2]),
    }


def reference(x_words, x_scales, w, b, gate, offs, pos1, pos2, pos3):
    idx = unstriped(offs)
    xq = unpack_weight(x_words, x_scales, "e4m3")[:, idx]
    y = by_expert(mxq(f64(w), 1, "e4m3"), xq)
    y = relu(y + np.repeat(f64(b), C, axis=1))
    return sum(f64(gate[r]) * y[:, unstriped(p)] for r, p in enumerate((pos1, pos2, pos3)))

@@ -1,0 +1,160 @@
+from contextlib import ExitStack
+
+import concourse.mybir as mybir
+
+K, T, E, C, N = 512, 640, 15, 128, 384
+TOP = 3
+SLOTS = E * C
+FLOPS = 2 * K * N * SLOTS
+
+F32 = mybir.dt.float32
+BF16 = mybir.dt.bfloat16
+I32 = mybir.dt.int32
+U32 = mybir.dt.uint32
+U16 = mybir.dt.uint16
+U8 = mybir.dt.uint8
+FP8X4 = mybir.dt.float8_e4m3fn_x4
+ALU = mybir.AluOpType
+ACT = mybir.ActivationFunctionType
+
+P = 128
+PACK = 4
+BLOCKS = N // P
+PER_COLUMN = 16
+GROUPS = [list(range(e, min(e + 2, E))) for e in range(0, E, 2)]
+ON_VECTOR = {(1, 0), (1, 2), (1, 4), (1, 8), (1, 12), (2, 0), (2, 4), (2, 8), (2, 12)}
+BYTES = 4 * (E * K * N + N * E + TOP * T + N * T) + K * T + 16 * T
+
+
+def tile_moe_pkd_lin_relu_kernel(tc, x_words, x_scales, w, b, gate, offs, pos1, pos2, pos3, out):
+    nc = tc.nc
+    with ExitStack() as ctx:
+        keep = ctx.enter_context(tc.tile_pool(name="keep", bufs=1))
+        ring = ctx.enter_context(tc.tile_pool(name="ring", bufs=4))
+        mix = ctx.enter_context(tc.tile_pool(name="mix", bufs=3))
+        psum = ctx.enter_context(tc.psum_pool(name="psum", bufs=8))
+
+        slot_list = keep.tile([P, SLOTS // PER_COLUMN], U16, name="slot_list")
+        back_lists = [keep.tile([P, T // PER_COLUMN], U16, name="back_list%d" % r) for r in range(TOP)]
+        words = keep.tile([P, T], I32, name="words", align_bytes=64)
+        scales = keep.tile([P, T], U8, name="scales", align_bytes=64)
+        bias = keep.tile([P, BLOCKS, 16], F32, name="bias")
+        gates = [keep.tile([P, T], F32, name="gate%d" % r) for r in range(TOP)]
+        y = [keep.tile([P, SLOTS], F32, name="y%d" % k) for k in range(BLOCKS)]
+        raw = {}
+
+        def load_w(k, e):
+            raw[k, e] = keep.tile([P, PACK, P], F32, name="raw%d_%d" % (k, e))
+            nc.sync.dma_start(out=raw[k, e][:], in_=w[e].rearrange("(p j) n -> p j n", j=PACK)[:, :, k * P:(k + 1) * P])
+
+        nc.vector.memset(scales[:].bitcast(I32), 0)
+        nc.sync.dma_start(out=slot_list[:], in_=offs)
+        nc.sync.dma_start(out=words[:], in_=x_words[0].rearrange("p t r -> p (t r)").bitcast(I32))
+        load_w(0, 0)
+        for r in range(4):
+            nc.sync.dma_start(out=scales[r:P:32, :].bitcast(I32), in_=x_scales[0, r:16:4, :].bitcast(I32))
+        load_w(0, 1)
+        nc.sync.dma_start(out=bias[:, :, 0:E], in_=b.rearrange("(k p) e -> p k e", p=P))
+        for e in range(2, E):
+            load_w(0, e)
+        for r, pos in enumerate((pos1, pos2, pos3)):
+            nc.sync.dma_start(out=back_lists[r][:], in_=pos)
+        for e in range(E):
+            if e in (1, 3, 5):
+                nc.sync.dma_start(out=gates[e // 2][:], in_=gate[e // 2, 0:P, :])
+            load_w(1, e)
+        for e in range(E):
+            load_w(2, e)
+
+        slot_words = {}
+        slot_scales = {}
+
+        def gather_tokens(g):
+            experts = GROUPS[g]
+            n = len(experts) * C
+            first = experts[0] * C // PER_COLUMN
+            entries = slot_list[:, first:first + n // PER_COLUMN]
+            slot_words[g] = keep.tile([P, n], U32, name="slot_words%d" % g, align_bytes=64)
+            slot_scales[g] = keep.tile([P, n], U8, name="slot_scales%d" % g, align_bytes=64)
+            nc.vector.tensor_copy(out=slot_words[g][:], in_=words[:].bitcast(U32).indirect(entries))
+            nc.vector.tensor_copy(out=slot_scales[g][:], in_=scales[:].indirect(entries))
+
+        rounded = {}
+        banks = {}
+
+        def round_w(k, g):
+            rounded[k, g] = ring.tile([P, 2, P, PACK], BF16, name="rounded", align_bytes=64)
+            for i, e in enumerate(GROUPS[g]):
+                dst = rounded[k, g][:, i, :, :].rearrange("p (c i) j -> p c j i", i=4)
+                src = raw[k, e][:].rearrange("p j (c i) -> p c j i", i=4)
+                if (k, e) in ON_VECTOR:
+                    nc.vector.tensor_copy(out=dst, in_=src)
+                else:
+                    nc.scalar.activation(out=dst, in_=src, func=ACT.Copy)
+
+        def multiply(k, g):
+            n = len(GROUPS[g]) * P
+            codes = ring.tile([P, 2 * P], U32, name="codes", align_bytes=64)
+            w_scales = ring.tile([P, 2 * P], U8, name="w_scales", align_bytes=64)
+            nc.vector.quantize_mx(
+                out=codes[:, 0:n].bitcast(FP8X4),
+                scales=w_scales[:, 0:n],
+                in_=rounded[k, g][:].rearrange("p i n j -> p (i n j)")[:, 0:n * PACK],
+            )
+            banks[k, g] = psum.tile([P, 2 * C], F32, name="bank")
+            for i in range(len(GROUPS[g])):
+                cols = slice(i * P, (i + 1) * P)
+                nc.tensor.matmul_mx(
+                    out=banks[k, g][:, cols],
+                    lhsT=codes[:, cols].bitcast(FP8X4),
+                    lhsT_scale=w_scales[:, cols],
+                    rhs=slot_words[g][:, cols].bitcast(FP8X4),
+                    rhs_scale=slot_scales[g][:, cols],
+                    start=True,
+                    stop=True,
+                )
+
+        def finish(k, g):
+            for i, e in enumerate(GROUPS[g]):
+                nc.scalar.activation(
+                    out=y[k][:, e * C:(e + 1) * C], in_=banks[k, g][:, i * C:(i + 1) * C], func=ACT.Relu, bias=bias[:, k, e:e + 1]
+                )
+
+        def combine_steps(k, t0, t1):
+            n = t1 - t0
+            parts = [mix.tile([P, n], F32, name="part%d" % r) for r in range(TOP)]
+            pair = mix.tile([P, n], F32, name="pair")
+            total = mix.tile([P, n], F32, name="total")
+
+            def fetch(r):
+                entries = back_lists[r][:, t0 // PER_COLUMN:t1 // PER_COLUMN]
+                nc.vector.tensor_tensor(out=parts[r][:], in0=y[k][:].indirect(entries), in1=gates[r][:, t0:t1], op=ALU.mult)
+
+            def add_two():
+                nc.vector.tensor_tensor(out=pair[:], in0=parts[0][:], in1=parts[1][:], op=ALU.add)
+
+            def add_third():
+                nc.vector.tensor_tensor(out=total[:], in0=pair[:], in1=parts[2][:], op=ALU.add)
+                nc.sync.dma_start(out=out[k * P:(k + 1) * P, t0:t1], in_=total[:])
+
+            return [lambda: fetch(0), lambda: fetch(1), lambda: fetch(2), add_two, add_third]
+
+        order = [(k, g) for k in range(BLOCKS) for g in range(len(GROUPS))]
+        pending = []
+        round_w(*order[0])
+        for s, (k, g) in enumerate(order):
+            if k == 0:
+                gather_tokens(g)
+            if s + 1 < len(order):
+                round_w(*order[s + 1])
+            multiply(k, g)
+            if s >= 1:
+                finish(*order[s - 1])
+            if g == 0 and k > 0:
+                pending = combine_steps(k - 1, 0, T)
+            elif 0 < g <= len(pending):
+                pending[g - 1]()
+        finish(*order[-1])
+        halves = [combine_steps(BLOCKS - 1, 0, T // 2), combine_steps(BLOCKS - 1, T // 2, T)]
+        for h, step in ((0, 0), (0, 1), (0, 2), (0, 3), (1, 0), (0, 4), (1, 1), (1, 2), (1, 3), (1, 4)):
+            halves[h][step]()

@@ -22,7 +22,9 @@ PACK = 4
 BLOCKS = N // P
 PER_COLUMN = 16
 GROUPS = [list(range(e, min(e + 2, E))) for e in range(0, E, 2)]
-ON_VECTOR = {(1, 0), (1, 2), (1, 4), (1, 8), (1, 12), (2, 0), (2, 4), (2, 8), (2, 12)}
+ON_VECTOR = {(1, 0), (1, 4), (1, 8), (1, 12), (2, 0), (2, 4), (2, 8), (2, 12)}
+SHELF = 4 * T
+GATE_AT = (1, 3, 4, 5, 6)
 BYTES = 4 * (E * K * N + N * E + TOP * T + N * T) + K * T + 16 * T
 
 
@@ -31,7 +33,7 @@ def tile_moe_pkd_lin_relu_kernel(tc, x_words, x_scales, w, b, gate, offs, pos1, 
     with ExitStack() as ctx:
         keep = ctx.enter_context(tc.tile_pool(name="keep", bufs=1))
         ring = ctx.enter_context(tc.tile_pool(name="ring", bufs=4))
-        mix = ctx.enter_context(tc.tile_pool(name="mix", bufs=3))
+        stage = ctx.enter_context(tc.tile_pool(name="stage", bufs=1))
         psum = ctx.enter_context(tc.psum_pool(name="psum", bufs=8))
 
         slot_list = keep.tile([P, SLOTS // PER_COLUMN], U16, name="slot_list")
@@ -66,6 +68,9 @@ def tile_moe_pkd_lin_relu_kernel(tc, x_words, x_scales, w, b, gate, offs, pos1, 
         for e in range(E):
             load_w(2, e)
 
+        def shelf(k, g):
+            return (k * len(GROUPS) + g) * SHELF
+
         slot_words = {}
         slot_scales = {}
 
@@ -74,8 +79,9 @@ def tile_moe_pkd_lin_relu_kernel(tc, x_words, x_scales, w, b, gate, offs, pos1, 
             n = len(experts) * C
             first = experts[0] * C // PER_COLUMN
             entries = slot_list[:, first:first + n // PER_COLUMN]
-            slot_words[g] = keep.tile([P, n], U32, name="slot_words%d" % g, align_bytes=64)
-            slot_scales[g] = keep.tile([P, n], U8, name="slot_scales%d" % g, align_bytes=64)
+            base = shelf(0, g - 2) if g >= 2 else shelf(BLOCKS, g)
+            slot_words[g] = stage.tile([P, n], U32, name="slot_words%d" % g, align_bytes=64, offset=base)
+            slot_scales[g] = stage.tile([P, n], U8, name="slot_scales%d" % g, align_bytes=64, offset=base + 4 * 2 * C)
             nc.vector.tensor_copy(out=slot_words[g][:], in_=words[:].bitcast(U32).indirect(entries))
             nc.vector.tensor_copy(out=slot_scales[g][:], in_=scales[:].indirect(entries))
 
@@ -83,7 +89,7 @@ def tile_moe_pkd_lin_relu_kernel(tc, x_words, x_scales, w, b, gate, offs, pos1, 
         banks = {}
 
         def round_w(k, g):
-            rounded[k, g] = ring.tile([P, 2, P, PACK], BF16, name="rounded", align_bytes=64)
+            rounded[k, g] = stage.tile([P, 2, P, PACK], BF16, name="rounded%d_%d" % (k, g), align_bytes=64, offset=shelf(k, g))
             for i, e in enumerate(GROUPS[g]):
                 dst = rounded[k, g][:, i, :, :].rearrange("p (c i) j -> p c j i", i=4)
                 src = raw[k, e][:].rearrange("p j (c i) -> p c j i", i=4)
@@ -122,9 +128,11 @@ def tile_moe_pkd_lin_relu_kernel(tc, x_words, x_scales, w, b, gate, offs, pos1, 
 
         def combine_steps(k, t0, t1):
             n = t1 - t0
-            parts = [mix.tile([P, n], F32, name="part%d" % r) for r in range(TOP)]
-            pair = mix.tile([P, n], F32, name="pair")
-            total = mix.tile([P, n], F32, name="total")
+            if k + 1 < BLOCKS:
+                tiles = [stage.tile([P, n], F32, name="mix%d_%d" % (k, i), align_bytes=64, offset=shelf(k + 1, GATE_AT[i])) for i in range(5)]
+            else:
+                tiles = [keep.tile([P, n], F32, name="tail%d_%d" % (t0, i)) for i in range(5)]
+            parts, pair, total = tiles[0:3], tiles[3], tiles[4]
 
             def fetch(r):
                 entries = back_lists[r][:, t0 // PER_COLUMN:t1 // PER_COLUMN]
@@ -152,8 +160,8 @@ def tile_moe_pkd_lin_relu_kernel(tc, x_words, x_scales, w, b, gate, offs, pos1, 
                 finish(*order[s - 1])
             if g == 0 and k > 0:
                 pending = combine_steps(k - 1, 0, T)
-            elif 0 < g <= len(pending):
-                pending[g - 1]()
+            if k > 0 and g in GATE_AT:
+                pending[GATE_AT.index(g)]()
         finish(*order[-1])
         halves = [combine_steps(BLOCKS - 1, 0, T // 2), combine_steps(BLOCKS - 1, T // 2, T)]
         for h, step in ((0, 0), (0, 1), (0, 2), (0, 3), (1, 0), (0, 4), (1, 1), (1, 2), (1, 3), (1, 4)):

@@ -1,11 +1,13 @@
 from contextlib import ExitStack
 
 import concourse.mybir as mybir
+from concourse.masks import make_identity
 
 K, T, E, C, N = 512, 640, 15, 128, 384
 TOP = 3
 SLOTS = E * C
 FLOPS = 2 * K * N * SLOTS
+BYTES = 4 * (E * K * N + N * E + TOP * T + N * T) + K * T + 16 * T
 
 F32 = mybir.dt.float32
 BF16 = mybir.dt.bfloat16
@@ -21,20 +23,23 @@ P = 128
 PACK = 4
 BLOCKS = N // P
 PER_COLUMN = 16
-GROUPS = [list(range(e, min(e + 2, E))) for e in range(0, E, 2)]
-ON_VECTOR = {(1, 0), (1, 4), (1, 8), (1, 12), (2, 0), (2, 4), (2, 8), (2, 12)}
-SHELF = 4 * T
-GATE_AT = (1, 3, 4, 5, 6)
-BYTES = 4 * (E * K * N + N * E + TOP * T + N * T) + K * T + 16 * T
+PAIRS = [list(range(e, min(e + 2, E))) for e in range(0, E, 2)]
+ON_VECTOR = {7, 9, 11, 13, 14, 15}
+SHELF = 4 * PACK * 2 * P
+FETCH_AFTER = {(0, 1): 16, (0, 2): 17, (1, 0): 18, (1, 1): 20, (1, 2): 22}
+TRIO = 3
+GATHER_AFTER = {2: 1, 3: 3, 4: 5}
+RUN = 4
 
 
 def tile_moe_pkd_lin_relu_kernel(tc, x_words, x_scales, w, b, gate, offs, pos1, pos2, pos3, out):
     nc = tc.nc
     with ExitStack() as ctx:
         keep = ctx.enter_context(tc.tile_pool(name="keep", bufs=1))
+        shelves = ctx.enter_context(tc.tile_pool(name="shelves", bufs=1))
         ring = ctx.enter_context(tc.tile_pool(name="ring", bufs=4))
-        stage = ctx.enter_context(tc.tile_pool(name="stage", bufs=1))
-        psum = ctx.enter_context(tc.psum_pool(name="psum", bufs=8))
+        psum = ctx.enter_context(tc.psum_pool(name="psum", bufs=4))
+        psum_mix = ctx.enter_context(tc.psum_pool(name="psum_mix", bufs=1))
 
         slot_list = keep.tile([P, SLOTS // PER_COLUMN], U16, name="slot_list")
         back_lists = [keep.tile([P, T // PER_COLUMN], U16, name="back_list%d" % r) for r in range(TOP)]
@@ -43,95 +48,113 @@ def tile_moe_pkd_lin_relu_kernel(tc, x_words, x_scales, w, b, gate, offs, pos1, 
         bias = keep.tile([P, BLOCKS, 16], F32, name="bias")
         gates = [keep.tile([P, T], F32, name="gate%d" % r) for r in range(TOP)]
         y = [keep.tile([P, SLOTS], F32, name="y%d" % k) for k in range(BLOCKS)]
-        raw = {}
 
-        def load_w(k, e):
-            raw[k, e] = keep.tile([P, PACK, P], F32, name="raw%d_%d" % (k, e))
-            nc.sync.dma_start(out=raw[k, e][:], in_=w[e].rearrange("(p j) n -> p j n", j=PACK)[:, :, k * P:(k + 1) * P])
+        whole = 15
+        units = [[(e, 0), (e, 1)] for e in range(whole)]
+        for k in range(2):
+            units.extend([(e, k) for e in range(e0, min(e0 + 2, E))] for e0 in range(whole, E, 2))
+        units.extend([(e, 2) for e in pair] for pair in PAIRS)
+        last_of = [max(u for u, unit in enumerate(units) if unit[-1][1] == k or unit[0][1] == k) for k in range(BLOCKS)]
+        raw = [
+            shelves.tile([P, PACK, len(unit) * P], F32, name="raw%d" % u, align_bytes=64, offset=u * SHELF)
+            for u, unit in enumerate(units)
+        ]
 
+        def rows(e):
+            return w[e].rearrange("(p j) n -> p j n", j=PACK)
+
+        def load_unit(u):
+            if u < whole:
+                nc.sync.dma_start(out=raw[u][:], in_=rows(u)[:, :, 0:2 * P])
+            else:
+                for i, (e, k) in enumerate(units[u]):
+                    nc.sync.dma_start(out=raw[u][:, :, i * P:(i + 1) * P], in_=rows(e)[:, :, k * P:(k + 1) * P])
+
+        identity = keep.tile([P, P], F32, name="identity")
+        make_identity(nc, identity[:])
         nc.vector.memset(scales[:].bitcast(I32), 0)
         nc.sync.dma_start(out=slot_list[:], in_=offs)
         nc.sync.dma_start(out=words[:], in_=x_words[0].rearrange("p t r -> p (t r)").bitcast(I32))
-        load_w(0, 0)
+        load_unit(0)
         for r in range(4):
             nc.sync.dma_start(out=scales[r:P:32, :].bitcast(I32), in_=x_scales[0, r:16:4, :].bitcast(I32))
-        load_w(0, 1)
+        load_unit(1)
         nc.sync.dma_start(out=bias[:, :, 0:E], in_=b.rearrange("(k p) e -> p k e", p=P))
-        for e in range(2, E):
-            load_w(0, e)
-        for r, pos in enumerate((pos1, pos2, pos3)):
-            nc.sync.dma_start(out=back_lists[r][:], in_=pos)
-        for e in range(E):
-            if e in (1, 3, 5):
-                nc.sync.dma_start(out=gates[e // 2][:], in_=gate[e // 2, 0:P, :])
-            load_w(1, e)
-        for e in range(E):
-            load_w(2, e)
-
-        def shelf(k, g):
-            return (k * len(GROUPS) + g) * SHELF
+        for u in range(2, len(units)):
+            load_unit(u)
+            if u == last_of[0] - 1:
+                for r, pos in enumerate((pos1, pos2, pos3)):
+                    nc.sync.dma_start(out=back_lists[r][:], in_=pos)
+            r = u - last_of[0] - 1
+            if 0 <= r < TOP:
+                nc.sync.dma_start(out=gates[r][:], in_=gate[r, 0:P, :])
 
         slot_words = {}
         slot_scales = {}
 
         def gather_tokens(g):
-            experts = GROUPS[g]
-            n = len(experts) * C
-            first = experts[0] * C // PER_COLUMN
-            entries = slot_list[:, first:first + n // PER_COLUMN]
-            base = shelf(0, g - 2) if g >= 2 else shelf(BLOCKS, g)
-            slot_words[g] = stage.tile([P, n], U32, name="slot_words%d" % g, align_bytes=64, offset=base)
-            slot_scales[g] = stage.tile([P, n], U8, name="slot_scales%d" % g, align_bytes=64, offset=base + 4 * 2 * C)
+            n = TRIO * C
+            entries = slot_list[:, g * n // PER_COLUMN:(g + 1) * n // PER_COLUMN]
+            base = (GATHER_AFTER[g] if g in GATHER_AFTER else len(units) + g) * SHELF
+            slot_words[g] = shelves.tile([P, n], U32, name="slot_words%d" % g, align_bytes=64, offset=base)
+            slot_scales[g] = shelves.tile([P, n], U8, name="slot_scales%d" % g, align_bytes=64, offset=base + 4 * n)
             nc.vector.tensor_copy(out=slot_words[g][:], in_=words[:].bitcast(U32).indirect(entries))
             nc.vector.tensor_copy(out=slot_scales[g][:], in_=scales[:].indirect(entries))
 
+        batches = [[0, 1], [2, 3], [4, 5], [6, 7], [8, 9], [10, 11], [12, 13], [14], [15, 16], [17, 18], [19, 20], [21], [22]]
+        batch_of = {u: s for s, batch in enumerate(batches) for u in batch}
+        pieces = [[piece for u in batch for piece in units[u]] for batch in batches]
         rounded = {}
         banks = {}
 
-        def round_w(k, g):
-            rounded[k, g] = stage.tile([P, 2, P, PACK], BF16, name="rounded%d_%d" % (k, g), align_bytes=64, offset=shelf(k, g))
-            for i, e in enumerate(GROUPS[g]):
-                dst = rounded[k, g][:, i, :, :].rearrange("p (c i) j -> p c j i", i=4)
-                src = raw[k, e][:].rearrange("p j (c i) -> p c j i", i=4)
-                if (k, e) in ON_VECTOR:
-                    nc.vector.tensor_copy(out=dst, in_=src)
-                else:
-                    nc.scalar.activation(out=dst, in_=src, func=ACT.Copy)
+        def round_w(u):
+            s = batch_of[u]
+            if s not in rounded:
+                rounded[s] = ring.tile([P, len(pieces[s]) * P, PACK], BF16, name="rounded", align_bytes=64)
+            first = batches[s].index(u) * 2 * P
+            dst = rounded[s][:, first:first + len(units[u]) * P, :].rearrange("p (c i) j -> p c j i", i=RUN)
+            src = raw[u][:].rearrange("p j (c i) -> p c j i", i=RUN)
+            if u in ON_VECTOR:
+                nc.vector.tensor_copy(out=dst, in_=src)
+            else:
+                nc.scalar.activation(out=dst, in_=src, func=ACT.Copy)
 
-        def multiply(k, g):
-            n = len(GROUPS[g]) * P
-            codes = ring.tile([P, 2 * P], U32, name="codes", align_bytes=64)
-            w_scales = ring.tile([P, 2 * P], U8, name="w_scales", align_bytes=64)
+        def multiply(s):
+            n = len(pieces[s]) * P
+            codes = ring.tile([P, n], U32, name="codes", align_bytes=64)
+            w_scales = ring.tile([P, n], U8, name="w_scales", align_bytes=64)
             nc.vector.quantize_mx(
-                out=codes[:, 0:n].bitcast(FP8X4),
-                scales=w_scales[:, 0:n],
-                in_=rounded[k, g][:].rearrange("p i n j -> p (i n j)")[:, 0:n * PACK],
+                out=codes[:].bitcast(FP8X4), scales=w_scales[:], in_=rounded[s][:].rearrange("p n j -> p (n j)")
             )
-            banks[k, g] = psum.tile([P, 2 * C], F32, name="bank")
-            for i in range(len(GROUPS[g])):
+            banks[s] = psum.tile([P, n], F32, name="bank")
+            for i, (e, k) in enumerate(pieces[s]):
                 cols = slice(i * P, (i + 1) * P)
+                slots = slice((e % TRIO) * C, (e % TRIO + 1) * C)
                 nc.tensor.matmul_mx(
-                    out=banks[k, g][:, cols],
+                    out=banks[s][:, cols],
                     lhsT=codes[:, cols].bitcast(FP8X4),
                     lhsT_scale=w_scales[:, cols],
-                    rhs=slot_words[g][:, cols].bitcast(FP8X4),
-                    rhs_scale=slot_scales[g][:, cols],
+                    rhs=slot_words[e // TRIO][:, slots].bitcast(FP8X4),
+                    rhs_scale=slot_scales[e // TRIO][:, slots],
                     start=True,
                     stop=True,
                 )
 
-        def finish(k, g):
-            for i, e in enumerate(GROUPS[g]):
+        def finish(s):
+            for i, (e, k) in enumerate(pieces[s]):
                 nc.scalar.activation(
-                    out=y[k][:, e * C:(e + 1) * C], in_=banks[k, g][:, i * C:(i + 1) * C], func=ACT.Relu, bias=bias[:, k, e:e + 1]
+                    out=y[k][:, e * C:(e + 1) * C], in_=banks[s][:, i * C:(i + 1) * C], func=ACT.Relu, bias=bias[:, k, e:e + 1]
                 )
 
-        def combine_steps(k, t0, t1):
+        def combine_steps(k, t0, t1, on_tensor):
             n = t1 - t0
-            if k + 1 < BLOCKS:
-                tiles = [stage.tile([P, n], F32, name="mix%d_%d" % (k, i), align_bytes=64, offset=shelf(k + 1, GATE_AT[i])) for i in range(5)]
-            else:
-                tiles = [keep.tile([P, n], F32, name="tail%d_%d" % (t0, i)) for i in range(5)]
+            tiles = []
+            for i in range(5):
+                if (k, i) in FETCH_AFTER:
+                    place = FETCH_AFTER[k, i] * SHELF
+                    tiles.append(shelves.tile([P, n], F32, name="mix%d_%d" % (k, i), align_bytes=64, offset=place))
+                else:
+                    tiles.append(keep.tile([P, n], F32, name="mix%d_%d_%d" % (k, i, t0)))
             parts, pair, total = tiles[0:3], tiles[3], tiles[4]
 
             def fetch(r):
@@ -145,24 +168,57 @@ def tile_moe_pkd_lin_relu_kernel(tc, x_words, x_scales, w, b, gate, offs, pos1, 
                 nc.vector.tensor_tensor(out=total[:], in0=pair[:], in1=parts[2][:], op=ALU.add)
                 nc.sync.dma_start(out=out[k * P:(k + 1) * P, t0:t1], in_=total[:])
 
+            spans = [(c0, min(c0 + 4 * P, n)) for c0 in range(0, n, 4 * P)]
+
+            sums = {}
+
+            def add_turned():
+                for h, (c0, c1) in enumerate(spans):
+                    sums[h] = psum_mix.tile([P, c1 - c0], F32, name="sums%d" % h, tag="mix%d_%d" % (k, h))
+                    for c in range(c0, c1, P):
+                        for r in range(TOP):
+                            nc.tensor.matmul(
+                                out=sums[h][:, c - c0:c - c0 + P], lhsT=parts[r][:, c:c + P], rhs=identity[:],
+                                is_transpose=True, start=(r == 0), stop=(r == TOP - 1),
+                            )
+
+            def turn_back():
+                for h, (c0, c1) in enumerate(spans):
+                    nc.scalar.copy(out=pair[:, c0:c1], in_=sums[h][:])
+                for h, (c0, c1) in enumerate(spans):
+                    back = psum_mix.tile([P, c1 - c0], F32, name="back%d" % h, tag="mix%d_%d" % (k, h))
+                    for c in range(c0, c1, P):
+                        nc.tensor.transpose(back[:, c - c0:c - c0 + P], pair[:, c:c + P], identity[:])
+                    nc.scalar.copy(out=total[:, c0:c1], in_=back[:])
+                nc.scalar.dma_start(out=out[k * P:(k + 1) * P, t0:t1], in_=total[:])
+
+            if on_tensor:
+                return [lambda: fetch(0), lambda: fetch(1), lambda: fetch(2), add_turned, turn_back]
             return [lambda: fetch(0), lambda: fetch(1), lambda: fetch(2), add_two, add_third]
 
-        order = [(k, g) for k in range(BLOCKS) for g in range(len(GROUPS))]
-        pending = []
-        round_w(*order[0])
-        for s, (k, g) in enumerate(order):
-            if k == 0:
+        early = [combine_steps(0, 0, T, True), combine_steps(1, 0, T, True)]
+        after = {15: [(0, 0)], 16: [(0, 1)], 17: [(0, 2)], 18: [(1, 0), (0, 3)], 20: [(1, 1)], 22: [(1, 2), (0, 4), (1, 3), (1, 4)]}
+        for g in range(E // TRIO):
+            if g not in GATHER_AFTER:
                 gather_tokens(g)
-            if s + 1 < len(order):
-                round_w(*order[s + 1])
-            multiply(k, g)
-            if s >= 1:
-                finish(*order[s - 1])
-            if g == 0 and k > 0:
-                pending = combine_steps(k - 1, 0, T)
-            if k > 0 and g in GATE_AT:
-                pending[GATE_AT.index(g)]()
-        finish(*order[-1])
-        halves = [combine_steps(BLOCKS - 1, 0, T // 2), combine_steps(BLOCKS - 1, T // 2, T)]
-        for h, step in ((0, 0), (0, 1), (0, 2), (0, 3), (1, 0), (0, 4), (1, 1), (1, 2), (1, 3), (1, 4)):
+        closing = [batch_of[u] for u in last_of]
+        begun = 0
+        for s, batch in enumerate(batches):
+            stop = min(batches[v][-1] for v in closing if v >= s)
+            while begun <= min(batch[-1] + 1, stop):
+                round_w(begun)
+                begun = begun + 1
+            multiply(s)
+            for g, u in GATHER_AFTER.items():
+                if u in batch:
+                    gather_tokens(g)
+            if s and s - 1 not in closing:
+                finish(s - 1)
+            if s in closing:
+                finish(s)
+            for u in batch:
+                for k, step in after.get(u, ()):
+                    early[k][step]()
+        halves = [combine_steps(BLOCKS - 1, 0, 320, False), combine_steps(BLOCKS - 1, 320, T, False)]
+        for h, step in ((0, 0), (0, 1), (1, 0), (0, 3), (1, 1), (0, 2), (1, 3), (0, 4), (1, 2), (1, 4)):
             halves[h][step]()

@@ -7,7 +7,7 @@ K, T, E, C, N = 512, 640, 15, 128, 384
 TOP = 3
 SLOTS = E * C
 FLOPS = 2 * K * N * SLOTS
-BYTES = 4 * (E * K * N + N * E + TOP * T + N * T) + K * T + 16 * T
+BYTES = 4 * (E * K * N + N * E + TOP * T + N * T) + K * T + (K // 32) * T
 
 F32 = mybir.dt.float32
 BF16 = mybir.dt.bfloat16
@@ -22,14 +22,32 @@ ACT = mybir.ActivationFunctionType
 P = 128
 PACK = 4
 BLOCKS = N // P
+BANK = 512
 PER_COLUMN = 16
-PAIRS = [list(range(e, min(e + 2, E))) for e in range(0, E, 2)]
-ON_VECTOR = {7, 9, 11, 13, 14, 15}
-SHELF = 4 * PACK * 2 * P
-FETCH_AFTER = {(0, 1): 16, (0, 2): 17, (1, 0): 18, (1, 1): 20, (1, 2): 22}
+
+CHUNKS = [[(e, 0), (e, 1)] for e in range(E)] + [
+    [(e, 2) for e in range(first, min(first + 2, E))] for first in range(0, E, 2)
+]
+LAST = len(CHUNKS) - 1
+BATCHES = (
+    [[u, u + 1] for u in range(0, E - 1, 2)]
+    + [[E - 1]]
+    + [[u, u + 1] for u in range(E, LAST - 1, 2)]
+    + [[LAST - 1], [LAST]]
+)
+SWEEP_ENDS = (E - 1, LAST)
+
+VECTOR_ROUNDS_FROM = 7
+ON_VECTOR = set(range(VECTOR_ROUNDS_FROM, E + 1, 2)) | {E - 1}
+
+RUN = 2
 TRIO = 3
-GATHER_AFTER = {2: 1, 3: 3, 4: 5}
-RUN = 4
+
+SHELF = 4 * PACK * 2 * P
+GATHER_AFTER = {g: 2 * g - 3 for g in range(2, E // TRIO)}
+FETCH_ORDER = [(k, r) for k in range(BLOCKS - 1) for r in range(TOP)]
+FETCH_WITH = dict(zip(FETCH_ORDER, (E, E + 1, E + 2, E + 3, LAST - 2, LAST)))
+SUM_WITH = E + 3
 
 
 def tile_moe_pkd_lin_relu_kernel(tc, x_words, x_scales, w, b, gate, offs, pos1, pos2, pos3, out):
@@ -45,49 +63,40 @@ def tile_moe_pkd_lin_relu_kernel(tc, x_words, x_scales, w, b, gate, offs, pos1, 
         back_lists = [keep.tile([P, T // PER_COLUMN], U16, name="back_list%d" % r) for r in range(TOP)]
         words = keep.tile([P, T], I32, name="words", align_bytes=64)
         scales = keep.tile([P, T], U8, name="scales", align_bytes=64)
-        bias = keep.tile([P, BLOCKS, 16], F32, name="bias")
+        bias = keep.tile([P, BLOCKS, E + 1], F32, name="bias")
         gates = [keep.tile([P, T], F32, name="gate%d" % r) for r in range(TOP)]
         y = [keep.tile([P, SLOTS], F32, name="y%d" % k) for k in range(BLOCKS)]
-
-        whole = 15
-        units = [[(e, 0), (e, 1)] for e in range(whole)]
-        for k in range(2):
-            units.extend([(e, k) for e in range(e0, min(e0 + 2, E))] for e0 in range(whole, E, 2))
-        units.extend([(e, 2) for e in pair] for pair in PAIRS)
-        last_of = [max(u for u, unit in enumerate(units) if unit[-1][1] == k or unit[0][1] == k) for k in range(BLOCKS)]
         raw = [
-            shelves.tile([P, PACK, len(unit) * P], F32, name="raw%d" % u, align_bytes=64, offset=u * SHELF)
-            for u, unit in enumerate(units)
+            shelves.tile([P, PACK, len(chunk) * P], F32, name="raw%d" % u, align_bytes=64, offset=u * SHELF)
+            for u, chunk in enumerate(CHUNKS)
         ]
 
-        def rows(e):
-            return w[e].rearrange("(p j) n -> p j n", j=PACK)
-
-        def load_unit(u):
-            if u < whole:
-                nc.sync.dma_start(out=raw[u][:], in_=rows(u)[:, :, 0:2 * P])
+        def load_chunk(u):
+            if u < E:
+                nc.sync.dma_start(out=raw[u][:], in_=w[u].rearrange("(p j) n -> p j n", j=PACK)[:, :, 0:2 * P])
             else:
-                for i, (e, k) in enumerate(units[u]):
-                    nc.sync.dma_start(out=raw[u][:, :, i * P:(i + 1) * P], in_=rows(e)[:, :, k * P:(k + 1) * P])
+                for i, (e, k) in enumerate(CHUNKS[u]):
+                    columns = w[e].rearrange("(p j) n -> p j n", j=PACK)[:, :, k * P:(k + 1) * P]
+                    nc.sync.dma_start(out=raw[u][:, :, i * P:(i + 1) * P], in_=columns)
 
         identity = keep.tile([P, P], F32, name="identity")
         make_identity(nc, identity[:])
+
         nc.vector.memset(scales[:].bitcast(I32), 0)
         nc.sync.dma_start(out=slot_list[:], in_=offs)
         nc.sync.dma_start(out=words[:], in_=x_words[0].rearrange("p t r -> p (t r)").bitcast(I32))
-        load_unit(0)
+        load_chunk(0)
         for r in range(4):
             nc.sync.dma_start(out=scales[r:P:32, :].bitcast(I32), in_=x_scales[0, r:16:4, :].bitcast(I32))
-        load_unit(1)
+        load_chunk(1)
         nc.sync.dma_start(out=bias[:, :, 0:E], in_=b.rearrange("(k p) e -> p k e", p=P))
-        for u in range(2, len(units)):
-            load_unit(u)
-            if u == last_of[0] - 1:
-                for r, pos in enumerate((pos1, pos2, pos3)):
-                    nc.sync.dma_start(out=back_lists[r][:], in_=pos)
-            r = u - last_of[0] - 1
-            if 0 <= r < TOP:
-                nc.sync.dma_start(out=gates[r][:], in_=gate[r, 0:P, :])
+        for u in range(2, len(CHUNKS)):
+            load_chunk(u)
+            if u == E - 2:
+                for back_list, pos in zip(back_lists, (pos1, pos2, pos3)):
+                    nc.sync.dma_start(out=back_list[:], in_=pos)
+            if E <= u < E + TOP:
+                nc.sync.dma_start(out=gates[u - E][:], in_=gate[u - E, 0:P, :])
 
         slot_words = {}
         slot_scales = {}
@@ -95,24 +104,23 @@ def tile_moe_pkd_lin_relu_kernel(tc, x_words, x_scales, w, b, gate, offs, pos1, 
         def gather_tokens(g):
             n = TRIO * C
             entries = slot_list[:, g * n // PER_COLUMN:(g + 1) * n // PER_COLUMN]
-            base = (GATHER_AFTER[g] if g in GATHER_AFTER else len(units) + g) * SHELF
-            slot_words[g] = shelves.tile([P, n], U32, name="slot_words%d" % g, align_bytes=64, offset=base)
-            slot_scales[g] = shelves.tile([P, n], U8, name="slot_scales%d" % g, align_bytes=64, offset=base + 4 * n)
+            place = GATHER_AFTER.get(g, len(CHUNKS) + g) * SHELF
+            slot_words[g] = shelves.tile([P, n], U32, name="slot_words%d" % g, align_bytes=64, offset=place)
+            slot_scales[g] = shelves.tile([P, n], U8, name="slot_scales%d" % g, align_bytes=64, offset=place + 4 * n)
             nc.vector.tensor_copy(out=slot_words[g][:], in_=words[:].bitcast(U32).indirect(entries))
             nc.vector.tensor_copy(out=slot_scales[g][:], in_=scales[:].indirect(entries))
 
-        batches = [[0, 1], [2, 3], [4, 5], [6, 7], [8, 9], [10, 11], [12, 13], [14], [15, 16], [17, 18], [19, 20], [21], [22]]
-        batch_of = {u: s for s, batch in enumerate(batches) for u in batch}
-        pieces = [[piece for u in batch for piece in units[u]] for batch in batches]
+        batch_of = {u: s for s, batch in enumerate(BATCHES) for u in batch}
+        pieces = [[piece for u in batch for piece in CHUNKS[u]] for batch in BATCHES]
         rounded = {}
         banks = {}
 
-        def round_w(u):
+        def round_chunk(u):
             s = batch_of[u]
             if s not in rounded:
                 rounded[s] = ring.tile([P, len(pieces[s]) * P, PACK], BF16, name="rounded", align_bytes=64)
-            first = batches[s].index(u) * 2 * P
-            dst = rounded[s][:, first:first + len(units[u]) * P, :].rearrange("p (c i) j -> p c j i", i=RUN)
+            first = BATCHES[s].index(u) * 2 * P
+            dst = rounded[s][:, first:first + len(CHUNKS[u]) * P, :].rearrange("p (c i) j -> p c j i", i=RUN)
             src = raw[u][:].rearrange("p j (c i) -> p c j i", i=RUN)
             if u in ON_VECTOR:
                 nc.vector.tensor_copy(out=dst, in_=src)
@@ -140,85 +148,106 @@ def tile_moe_pkd_lin_relu_kernel(tc, x_words, x_scales, w, b, gate, offs, pos1, 
                     stop=True,
                 )
 
-        def finish(s):
+        def activate(s):
             for i, (e, k) in enumerate(pieces[s]):
                 nc.scalar.activation(
                     out=y[k][:, e * C:(e + 1) * C], in_=banks[s][:, i * C:(i + 1) * C], func=ACT.Relu, bias=bias[:, k, e:e + 1]
                 )
 
-        def combine_steps(k, t0, t1, on_tensor):
-            n = t1 - t0
+        def combine_tiles(k, t0, t1):
             tiles = []
-            for i in range(5):
-                if (k, i) in FETCH_AFTER:
-                    place = FETCH_AFTER[k, i] * SHELF
-                    tiles.append(shelves.tile([P, n], F32, name="mix%d_%d" % (k, i), align_bytes=64, offset=place))
+            for i in range(TOP + 2):
+                if FETCH_WITH.get((k, i), E) > E:
+                    place = FETCH_WITH[k, i] * SHELF
+                    tiles.append(shelves.tile([P, t1 - t0], F32, name="mix%d_%d" % (k, i), align_bytes=64, offset=place))
                 else:
-                    tiles.append(keep.tile([P, n], F32, name="mix%d_%d_%d" % (k, i, t0)))
-            parts, pair, total = tiles[0:3], tiles[3], tiles[4]
+                    tiles.append(keep.tile([P, t1 - t0], F32, name="mix%d_%d_%d" % (k, i, t0)))
+            return {"k": k, "tokens": slice(t0, t1), "parts": tiles[:TOP], "interim": tiles[TOP], "total": tiles[TOP + 1]}
 
-            def fetch(r):
-                entries = back_lists[r][:, t0 // PER_COLUMN:t1 // PER_COLUMN]
-                nc.vector.tensor_tensor(out=parts[r][:], in0=y[k][:].indirect(entries), in1=gates[r][:, t0:t1], op=ALU.mult)
+        def fetch(job, r):
+            tokens = job["tokens"]
+            entries = back_lists[r][:, tokens.start // PER_COLUMN:tokens.stop // PER_COLUMN]
+            nc.vector.tensor_tensor(
+                out=job["parts"][r][:], in0=y[job["k"]][:].indirect(entries), in1=gates[r][:, tokens], op=ALU.mult
+            )
 
-            def add_two():
-                nc.vector.tensor_tensor(out=pair[:], in0=parts[0][:], in1=parts[1][:], op=ALU.add)
+        def out_rows(job):
+            return out[job["k"] * P:(job["k"] + 1) * P, job["tokens"]]
 
-            def add_third():
-                nc.vector.tensor_tensor(out=total[:], in0=pair[:], in1=parts[2][:], op=ALU.add)
-                nc.sync.dma_start(out=out[k * P:(k + 1) * P, t0:t1], in_=total[:])
+        spans = [(c0, min(c0 + BANK, T)) for c0 in range(0, T, BANK)]
+        sums = {}
 
-            spans = [(c0, min(c0 + 4 * P, n)) for c0 in range(0, n, 4 * P)]
+        def add_on_tensor(job):
+            k = job["k"]
+            for h, (c0, c1) in enumerate(spans):
+                sums[k, h] = psum_mix.tile([P, c1 - c0], F32, name="sums%d" % h, tag="mix%d_%d" % (k, h))
+                for c in range(c0, c1, P):
+                    for r in range(TOP):
+                        nc.tensor.matmul(
+                            out=sums[k, h][:, c - c0:c - c0 + P],
+                            lhsT=job["parts"][r][:, c:c + P],
+                            rhs=identity[:],
+                            is_transpose=True,
+                            start=(r == 0),
+                            stop=(r == TOP - 1),
+                        )
 
-            sums = {}
+        def turn_back_and_store(job):
+            k = job["k"]
+            for h, (c0, c1) in enumerate(spans):
+                nc.scalar.copy(out=job["interim"][:, c0:c1], in_=sums[k, h][:])
+            for h, (c0, c1) in enumerate(spans):
+                back = psum_mix.tile([P, c1 - c0], F32, name="back%d" % h, tag="mix%d_%d" % (k, h))
+                for c in range(c0, c1, P):
+                    nc.tensor.transpose(back[:, c - c0:c - c0 + P], job["interim"][:, c:c + P], identity[:])
+                nc.scalar.copy(out=job["total"][:, c0:c1], in_=back[:])
+            nc.scalar.dma_start(out=out_rows(job), in_=job["total"][:])
 
-            def add_turned():
-                for h, (c0, c1) in enumerate(spans):
-                    sums[h] = psum_mix.tile([P, c1 - c0], F32, name="sums%d" % h, tag="mix%d_%d" % (k, h))
-                    for c in range(c0, c1, P):
-                        for r in range(TOP):
-                            nc.tensor.matmul(
-                                out=sums[h][:, c - c0:c - c0 + P], lhsT=parts[r][:, c:c + P], rhs=identity[:],
-                                is_transpose=True, start=(r == 0), stop=(r == TOP - 1),
-                            )
+        def add_two(job):
+            nc.vector.tensor_tensor(out=job["interim"][:], in0=job["parts"][0][:], in1=job["parts"][1][:], op=ALU.add)
 
-            def turn_back():
-                for h, (c0, c1) in enumerate(spans):
-                    nc.scalar.copy(out=pair[:, c0:c1], in_=sums[h][:])
-                for h, (c0, c1) in enumerate(spans):
-                    back = psum_mix.tile([P, c1 - c0], F32, name="back%d" % h, tag="mix%d_%d" % (k, h))
-                    for c in range(c0, c1, P):
-                        nc.tensor.transpose(back[:, c - c0:c - c0 + P], pair[:, c:c + P], identity[:])
-                    nc.scalar.copy(out=total[:, c0:c1], in_=back[:])
-                nc.scalar.dma_start(out=out[k * P:(k + 1) * P, t0:t1], in_=total[:])
+        def add_third_and_store(job):
+            nc.vector.tensor_tensor(out=job["total"][:], in0=job["interim"][:], in1=job["parts"][2][:], op=ALU.add)
+            nc.sync.dma_start(out=out_rows(job), in_=job["total"][:])
 
-            if on_tensor:
-                return [lambda: fetch(0), lambda: fetch(1), lambda: fetch(2), add_turned, turn_back]
-            return [lambda: fetch(0), lambda: fetch(1), lambda: fetch(2), add_two, add_third]
-
-        early = [combine_steps(0, 0, T, True), combine_steps(1, 0, T, True)]
-        after = {15: [(0, 0)], 16: [(0, 1)], 17: [(0, 2)], 18: [(1, 0), (0, 3)], 20: [(1, 1)], 22: [(1, 2), (0, 4), (1, 3), (1, 4)]}
+        early = [combine_tiles(k, 0, T) for k in range(BLOCKS - 1)]
         for g in range(E // TRIO):
             if g not in GATHER_AFTER:
                 gather_tokens(g)
-        closing = [batch_of[u] for u in last_of]
+
         begun = 0
-        for s, batch in enumerate(batches):
-            stop = min(batches[v][-1] for v in closing if v >= s)
-            while begun <= min(batch[-1] + 1, stop):
-                round_w(begun)
+        for s, batch in enumerate(BATCHES):
+            sweep_end = min(u for u in SWEEP_ENDS if u >= batch[-1])
+            while begun <= min(batch[-1] + 1, sweep_end):
+                round_chunk(begun)
                 begun = begun + 1
             multiply(s)
             for g, u in GATHER_AFTER.items():
                 if u in batch:
                     gather_tokens(g)
-            if s and s - 1 not in closing:
-                finish(s - 1)
-            if s in closing:
-                finish(s)
-            for u in batch:
-                for k, step in after.get(u, ()):
-                    early[k][step]()
-        halves = [combine_steps(BLOCKS - 1, 0, 320, False), combine_steps(BLOCKS - 1, 320, T, False)]
-        for h, step in ((0, 0), (0, 1), (1, 0), (0, 3), (1, 1), (0, 2), (1, 3), (0, 4), (1, 2), (1, 4)):
-            halves[h][step]()
+            if s > 0 and BATCHES[s - 1][-1] not in SWEEP_ENDS:
+                activate(s - 1)
+            if batch[-1] in SWEEP_ENDS:
+                activate(s)
+            for (k, r), u in FETCH_WITH.items():
+                if u in batch:
+                    fetch(early[k], r)
+            if SUM_WITH in batch:
+                add_on_tensor(early[0])
+
+        turn_back_and_store(early[0])
+        add_on_tensor(early[1])
+        turn_back_and_store(early[1])
+
+        low = combine_tiles(BLOCKS - 1, 0, T // 2)
+        high = combine_tiles(BLOCKS - 1, T // 2, T)
+        fetch(low, 0)
+        fetch(low, 1)
+        fetch(high, 0)
+        add_two(low)
+        fetch(high, 1)
+        fetch(low, 2)
+        add_two(high)
+        add_third_and_store(low)
+        fetch(high, 2)
+        add_third_and_store(high)

from contextlib import ExitStack

import concourse.mybir as mybir
from concourse.masks import make_identity

K, T, E, C, N = 512, 640, 15, 128, 384
TOP = 3
SLOTS = E * C
FLOPS = 2 * K * N * SLOTS
BYTES = 4 * (E * K * N + N * E + TOP * T + N * T) + K * T + (K // 32) * T

F32 = mybir.dt.float32
BF16 = mybir.dt.bfloat16
I32 = mybir.dt.int32
U32 = mybir.dt.uint32
U16 = mybir.dt.uint16
U8 = mybir.dt.uint8
FP8X4 = mybir.dt.float8_e4m3fn_x4
ALU = mybir.AluOpType
ACT = mybir.ActivationFunctionType

P = 128
PACK = 4
BLOCKS = N // P
BANK = 512
PER_COLUMN = 16

CHUNKS = [[(e, 0), (e, 1)] for e in range(E)] + [
    [(e, 2) for e in range(first, min(first + 2, E))] for first in range(0, E, 2)
]
LAST = len(CHUNKS) - 1
BATCHES = (
    [[u, u + 1] for u in range(0, E - 1, 2)]
    + [[E - 1]]
    + [[u, u + 1] for u in range(E, LAST - 1, 2)]
    + [[LAST - 1], [LAST]]
)
SWEEP_ENDS = (E - 1, LAST)

VECTOR_ROUNDS_FROM = 7
ON_VECTOR = set(range(VECTOR_ROUNDS_FROM, E + 1, 2)) | {E - 1}

RUN = 2
TRIO = 3

SHELF = 4 * PACK * 2 * P
GATHER_AFTER = {g: 2 * g - 3 for g in range(2, E // TRIO)}
FETCH_ORDER = [(k, r) for k in range(BLOCKS - 1) for r in range(TOP)]
FETCH_WITH = dict(zip(FETCH_ORDER, (E, E + 1, E + 2, E + 3, LAST - 2, LAST)))
SUM_WITH = E + 3


def tile_moe_pkd_lin_relu_kernel(tc, x_words, x_scales, w, b, gate, offs, pos1, pos2, pos3, out):
    nc = tc.nc
    with ExitStack() as ctx:
        keep = ctx.enter_context(tc.tile_pool(name="keep", bufs=1))
        shelves = ctx.enter_context(tc.tile_pool(name="shelves", bufs=1))
        ring = ctx.enter_context(tc.tile_pool(name="ring", bufs=4))
        psum = ctx.enter_context(tc.psum_pool(name="psum", bufs=4))
        psum_mix = ctx.enter_context(tc.psum_pool(name="psum_mix", bufs=1))

        slot_list = keep.tile([P, SLOTS // PER_COLUMN], U16, name="slot_list")
        back_lists = [keep.tile([P, T // PER_COLUMN], U16, name="back_list%d" % r) for r in range(TOP)]
        words = keep.tile([P, T], I32, name="words", align_bytes=64)
        scales = keep.tile([P, T], U8, name="scales", align_bytes=64)
        bias = keep.tile([P, BLOCKS, E + 1], F32, name="bias")
        gates = [keep.tile([P, T], F32, name="gate%d" % r) for r in range(TOP)]
        y = [keep.tile([P, SLOTS], F32, name="y%d" % k) for k in range(BLOCKS)]
        raw = [
            shelves.tile([P, PACK, len(chunk) * P], F32, name="raw%d" % u, align_bytes=64, offset=u * SHELF)
            for u, chunk in enumerate(CHUNKS)
        ]

        def load_chunk(u):
            if u < E:
                nc.sync.dma_start(out=raw[u][:], in_=w[u].rearrange("(p j) n -> p j n", j=PACK)[:, :, 0:2 * P])
            else:
                for i, (e, k) in enumerate(CHUNKS[u]):
                    columns = w[e].rearrange("(p j) n -> p j n", j=PACK)[:, :, k * P:(k + 1) * P]
                    nc.sync.dma_start(out=raw[u][:, :, i * P:(i + 1) * P], in_=columns)

        identity = keep.tile([P, P], F32, name="identity")
        make_identity(nc, identity[:])

        nc.vector.memset(scales[:].bitcast(I32), 0)
        nc.sync.dma_start(out=slot_list[:], in_=offs)
        nc.sync.dma_start(out=words[:], in_=x_words[0].rearrange("p t r -> p (t r)").bitcast(I32))
        load_chunk(0)
        for r in range(4):
            nc.sync.dma_start(out=scales[r:P:32, :].bitcast(I32), in_=x_scales[0, r:16:4, :].bitcast(I32))
        load_chunk(1)
        nc.sync.dma_start(out=bias[:, :, 0:E], in_=b.rearrange("(k p) e -> p k e", p=P))
        for u in range(2, len(CHUNKS)):
            load_chunk(u)
            if u == E - 2:
                for back_list, pos in zip(back_lists, (pos1, pos2, pos3)):
                    nc.sync.dma_start(out=back_list[:], in_=pos)
            if E <= u < E + TOP:
                nc.sync.dma_start(out=gates[u - E][:], in_=gate[u - E, 0:P, :])

        slot_words = {}
        slot_scales = {}

        def gather_tokens(g):
            n = TRIO * C
            entries = slot_list[:, g * n // PER_COLUMN:(g + 1) * n // PER_COLUMN]
            place = GATHER_AFTER.get(g, len(CHUNKS) + g) * SHELF
            slot_words[g] = shelves.tile([P, n], U32, name="slot_words%d" % g, align_bytes=64, offset=place)
            slot_scales[g] = shelves.tile([P, n], U8, name="slot_scales%d" % g, align_bytes=64, offset=place + 4 * n)
            nc.vector.tensor_copy(out=slot_words[g][:], in_=words[:].bitcast(U32).indirect(entries))
            nc.vector.tensor_copy(out=slot_scales[g][:], in_=scales[:].indirect(entries))

        batch_of = {u: s for s, batch in enumerate(BATCHES) for u in batch}
        pieces = [[piece for u in batch for piece in CHUNKS[u]] for batch in BATCHES]
        rounded = {}
        banks = {}

        def round_chunk(u):
            s = batch_of[u]
            if s not in rounded:
                rounded[s] = ring.tile([P, len(pieces[s]) * P, PACK], BF16, name="rounded", align_bytes=64)
            first = BATCHES[s].index(u) * 2 * P
            dst = rounded[s][:, first:first + len(CHUNKS[u]) * P, :].rearrange("p (c i) j -> p c j i", i=RUN)
            src = raw[u][:].rearrange("p j (c i) -> p c j i", i=RUN)
            if u in ON_VECTOR:
                nc.vector.tensor_copy(out=dst, in_=src)
            else:
                nc.scalar.activation(out=dst, in_=src, func=ACT.Copy)

        def multiply(s):
            n = len(pieces[s]) * P
            codes = ring.tile([P, n], U32, name="codes", align_bytes=64)
            w_scales = ring.tile([P, n], U8, name="w_scales", align_bytes=64)
            nc.vector.quantize_mx(
                out=codes[:].bitcast(FP8X4), scales=w_scales[:], in_=rounded[s][:].rearrange("p n j -> p (n j)")
            )
            banks[s] = psum.tile([P, n], F32, name="bank")
            for i, (e, k) in enumerate(pieces[s]):
                cols = slice(i * P, (i + 1) * P)
                slots = slice((e % TRIO) * C, (e % TRIO + 1) * C)
                nc.tensor.matmul_mx(
                    out=banks[s][:, cols],
                    lhsT=codes[:, cols].bitcast(FP8X4),
                    lhsT_scale=w_scales[:, cols],
                    rhs=slot_words[e // TRIO][:, slots].bitcast(FP8X4),
                    rhs_scale=slot_scales[e // TRIO][:, slots],
                    start=True,
                    stop=True,
                )

        def activate(s):
            for i, (e, k) in enumerate(pieces[s]):
                nc.scalar.activation(
                    out=y[k][:, e * C:(e + 1) * C], in_=banks[s][:, i * C:(i + 1) * C], func=ACT.Relu, bias=bias[:, k, e:e + 1]
                )

        def combine_tiles(k, t0, t1):
            tiles = []
            for i in range(TOP + 2):
                if FETCH_WITH.get((k, i), E) > E:
                    place = FETCH_WITH[k, i] * SHELF
                    tiles.append(shelves.tile([P, t1 - t0], F32, name="mix%d_%d" % (k, i), align_bytes=64, offset=place))
                else:
                    tiles.append(keep.tile([P, t1 - t0], F32, name="mix%d_%d_%d" % (k, i, t0)))
            return {"k": k, "tokens": slice(t0, t1), "parts": tiles[:TOP], "interim": tiles[TOP], "total": tiles[TOP + 1]}

        def fetch(job, r):
            tokens = job["tokens"]
            entries = back_lists[r][:, tokens.start // PER_COLUMN:tokens.stop // PER_COLUMN]
            nc.vector.tensor_tensor(
                out=job["parts"][r][:], in0=y[job["k"]][:].indirect(entries), in1=gates[r][:, tokens], op=ALU.mult
            )

        def out_rows(job):
            return out[job["k"] * P:(job["k"] + 1) * P, job["tokens"]]

        spans = [(c0, min(c0 + BANK, T)) for c0 in range(0, T, BANK)]
        sums = {}

        def add_on_tensor(job):
            k = job["k"]
            for h, (c0, c1) in enumerate(spans):
                sums[k, h] = psum_mix.tile([P, c1 - c0], F32, name="sums%d" % h, tag="mix%d_%d" % (k, h))
                for c in range(c0, c1, P):
                    for r in range(TOP):
                        nc.tensor.matmul(
                            out=sums[k, h][:, c - c0:c - c0 + P],
                            lhsT=job["parts"][r][:, c:c + P],
                            rhs=identity[:],
                            is_transpose=True,
                            start=(r == 0),
                            stop=(r == TOP - 1),
                        )

        def turn_back_and_store(job):
            k = job["k"]
            for h, (c0, c1) in enumerate(spans):
                nc.scalar.copy(out=job["interim"][:, c0:c1], in_=sums[k, h][:])
            for h, (c0, c1) in enumerate(spans):
                back = psum_mix.tile([P, c1 - c0], F32, name="back%d" % h, tag="mix%d_%d" % (k, h))
                for c in range(c0, c1, P):
                    nc.tensor.transpose(back[:, c - c0:c - c0 + P], job["interim"][:, c:c + P], identity[:])
                nc.scalar.copy(out=job["total"][:, c0:c1], in_=back[:])
            nc.scalar.dma_start(out=out_rows(job), in_=job["total"][:])

        def add_two(job):
            nc.vector.tensor_tensor(out=job["interim"][:], in0=job["parts"][0][:], in1=job["parts"][1][:], op=ALU.add)

        def add_third_and_store(job):
            nc.vector.tensor_tensor(out=job["total"][:], in0=job["interim"][:], in1=job["parts"][2][:], op=ALU.add)
            nc.sync.dma_start(out=out_rows(job), in_=job["total"][:])

        early = [combine_tiles(k, 0, T) for k in range(BLOCKS - 1)]
        for g in range(E // TRIO):
            if g not in GATHER_AFTER:
                gather_tokens(g)

        begun = 0
        for s, batch in enumerate(BATCHES):
            sweep_end = min(u for u in SWEEP_ENDS if u >= batch[-1])
            while begun <= min(batch[-1] + 1, sweep_end):
                round_chunk(begun)
                begun = begun + 1
            multiply(s)
            for g, u in GATHER_AFTER.items():
                if u in batch:
                    gather_tokens(g)
            if s > 0 and BATCHES[s - 1][-1] not in SWEEP_ENDS:
                activate(s - 1)
            if batch[-1] in SWEEP_ENDS:
                activate(s)
            for (k, r), u in FETCH_WITH.items():
                if u in batch:
                    fetch(early[k], r)
            if SUM_WITH in batch:
                add_on_tensor(early[0])

        turn_back_and_store(early[0])
        add_on_tensor(early[1])
        turn_back_and_store(early[1])

        low = combine_tiles(BLOCKS - 1, 0, T // 2)
        high = combine_tiles(BLOCKS - 1, T // 2, T)
        fetch(low, 0)
        fetch(low, 1)
        fetch(high, 0)
        add_two(low)
        fetch(high, 1)
        fetch(low, 2)
        add_two(high)
        add_third_and_store(low)
        fetch(high, 2)
        add_third_and_store(high)
